import numpy as np
import ml_dtypes


def mxq(x, axis, fmt="e4m3"):
    dtype, down = {"e4m3": (ml_dtypes.float8_e4m3fn, 7), "e5m2": (ml_dtypes.float8_e5m2, 14)}[fmt]
    v = np.moveaxis(np.asarray(x, np.float32).astype(ml_dtypes.bfloat16).astype(np.float64), axis, -1)
    blocks = v.reshape(v.shape[:-1] + (-1, 32))
    amax = np.abs(blocks).max(-1, keepdims=True)
    byte = np.maximum(np.where(amax > 0, np.frexp(amax)[1] - 1 + 127, 0) - down, 1)
    scale = np.exp2(byte - 127.0)
    codes = (blocks / scale).astype(np.float32).astype(dtype).astype(np.float64)
    return np.moveaxis((codes * scale).reshape(v.shape), -1, axis)


WIDE = False


def mx_kscale(k):
    if not WIDE:
        return np.ones(k)
    levels = np.array([30, -30])
    if k % 512:
        return np.exp2(np.random.permutation(np.resize(levels, k // 32))).repeat(32)
    a = np.empty((k // 512, 16))
    for p in range(k // 512):
        a[p, :8] = np.random.permutation(np.resize(levels, 8))
        for g in range(8):
            far = levels[np.abs(levels - a[p, g]) >= 10]
            a[p, g + 8] = far[np.random.randint(len(far))]
    return np.exp2(a.ravel()).repeat(32)


def f64(x):
    return np.asarray(x).astype(np.float64)


def striped(idx):
    return np.tile(np.asarray(idx).reshape(-1, 16).T, (8, 1)).astype(np.uint16)


def unstriped(offs):
    return offs[:16].T.reshape(-1).astype(np.int64)


E2M1 = np.array([0.0, 0.5, 1.0, 1.5, 2.0, 3.0, 4.0, 6.0, -0.0, -0.5, -1.0, -1.5, -2.0, -3.0, -4.0, -6.0])


def pack_weight(w, fmt):
    k, n = w.shape
    w = f64(np.asarray(w, np.float32).astype(ml_dtypes.bfloat16)).reshape(k // 32, 32, n)
    amax = np.abs(w).max(1)
    if fmt in ("e4m3", "e5m2"):
        byte = np.frexp(amax)[1] - 1 + 127 - (7 if fmt == "e4m3" else 14)
    else:
        mant, ex = np.frexp(amax / 6.0)
        byte = np.where(mant > 0.5, ex, ex - 1) + 127
    byte = np.clip(np.where(amax > 0, byte, 1), 1, 254)
    scaled = (w * np.exp2(127.0 - byte)[:, None, :]).reshape(k, n).astype(np.float32)
    by_word = np.ascontiguousarray(scaled.reshape(k // 512, 128, 4, n).transpose(0, 1, 3, 2))
    if fmt in ("e4m3", "e5m2"):
        words = by_word.astype(ml_dtypes.float8_e4m3fn if fmt == "e4m3" else ml_dtypes.float8_e5m2).view(np.uint8)
    else:
        c = by_word.astype(ml_dtypes.float4_e2m1fn).view(np.uint8) & 0xF
        words = (c[..., 0::2] | (c[..., 1::2] << 4)).reshape(k // 512, 128, 2 * n)
    return np.ascontiguousarray(words), np.ascontiguousarray(byte.astype(np.uint8).reshape(k // 512, 16, n))


def unpack_weight(words, scales, fmt):
    g, _, n = scales.shape
    words = np.ascontiguousarray(words).reshape(g, 128, n, -1)
    if fmt in ("e4m3", "e5m2"):
        vals = words.view(ml_dtypes.float8_e4m3fn if fmt == "e4m3" else ml_dtypes.float8_e5m2).astype(np.float64)
    else:
        nib = np.empty((g, 128, n, 4), np.uint8)
        nib[..., 0::2] = words & 0xF
        nib[..., 1::2] = words >> 4
        vals = E2M1[nib]
    vals = vals * np.repeat(np.exp2(scales.astype(np.float64) - 127.0), 8, axis=1)[..., None]
    return vals.transpose(0, 1, 3, 2).reshape(g * 512, n)


def bf(x):
    return np.asarray(x, np.float32).astype(ml_dtypes.bfloat16)


def planes(Y):
    r, m = Y.shape
    b = f64(bf(Y)).reshape(r // 32, 32, m)
    amax = np.abs(b).max(1)
    byte = np.clip(np.where(amax > 0, np.frexp(amax)[1] - 1 + 127 - 7, 1), 1, 254)
    codes = (b * np.exp2(127.0 - byte)[:, None, :]).reshape(r, m).astype(np.float32).astype(ml_dtypes.float8_e4m3fn).view(np.uint8)
    words = codes.reshape(r // 512, 128, 4, m).transpose(0, 1, 3, 2)
    return np.ascontiguousarray(words), np.ascontiguousarray(byte.astype(np.uint8).reshape(r // 512, 16, m))


K, T, J, S, R, G, N, Q = 512, 1024, 256, 512, 512, 128, 512, 64


def setup_inputs():
    n = np.random.standard_normal
    idx = np.random.permutation(T)[:J]
    idx2 = np.random.permutation(S)[:J]
    fk = mx_kscale(K)
    fr = mx_kscale(R)
    wp = pack_weight(n((K, R)) * 1 / np.sqrt(K) * fk[:, None] * fr, "e5m2")
    wbp = pack_weight(n((R, N)) * 1 / np.sqrt(R) / fr[:, None], "e2m1")
    return {
        "xa": (n((K, T))).astype(np.float32),
        "xb": (n((K, S))).astype(np.float32),
        "hb": (np.random.uniform(0.2, 0.9, (K, 1))).astype(np.float32),
        "fk": (np.random.uniform(0.5, 2.0, (K, 1)) / fk[:, None]).astype(np.float32),
        "w_words": wp[0],
        "w_scales": wp[1],
        "wb_words": wbp[0],
        "wb_scales": wbp[1],
        "rw": (np.random.uniform(0.5, 2.0, (1, G))).astype(np.float32),
        "qw": (np.random.uniform(0.5, 2.0, (1, Q))).astype(np.float32),
        "offs": striped(idx),
        "offs2": striped(idx2),
    }


def reference(xa, xb, hb, fk, w_words, w_scales, wb_words, wb_scales, rw, qw, offs, offs2):
    idx = unstriped(offs)
    idx2 = unstriped(offs2)
    wu = unpack_weight(w_words, w_scales, "e5m2")
    wbu = unpack_weight(wb_words, wb_scales, "e2m1")
    u = (f64(xa)[:, idx] - np.minimum(f64(xb)[:, idx2], f64(hb))) * f64(fk)
    uq = mxq(u, 0, "e5m2")
    a = wu.T @ uq
    hid = a.reshape(R, G, J // G).max(axis=2)
    hidq = mxq(hid, 0, "e5m2")
    p = wbu.T @ hidq
    y = (p * f64(rw)).reshape(N, Q, G // Q).sum(axis=2) * f64(qw)
    words, scales = planes(y)
    return y, words, scales

@@ -1,0 +1,224 @@
+from contextlib import ExitStack
+
+import concourse.mybir as mybir
+
+K, T, J, S, R, G, N, Q = 512, 1024, 256, 512, 512, 128, 512, 64
+FLOPS = 2 * K * R * J + 2 * R * N * G
+
+F32 = mybir.dt.float32
+BF16 = mybir.dt.bfloat16
+I32 = mybir.dt.int32
+U32 = mybir.dt.uint32
+U16 = mybir.dt.uint16
+U8 = mybir.dt.uint8
+E5M2 = mybir.dt.float8_e5m2_x4
+E4M3 = mybir.dt.float8_e4m3fn_x4
+E2M1 = mybir.dt.float4_e2m1fn_x4
+ALU = mybir.AluOpType
+COPY = mybir.ActivationFunctionType.Copy
+AXIS_X = mybir.AxisListType.X
+
+P = 128
+PACK = 4
+HALF = J // 2
+
+
+def load_scale_rows(queue, tile, scales):
+    for quad in range(4):
+        queue.dma_start(
+            out=tile[32 * quad : 32 * quad + 4, :].bitcast(I32),
+            in_=scales[0, 4 * quad : 4 * quad + 4, :].bitcast(I32),
+        )
+
+
+def tile_list_boundedgaps_pooled_groupsums_pl_kernel(
+    tc, xa, xb, hb, fk, w_words, w_scales, wb_words, wb_scales, rw, qw, offs, offs2, out_0, out_1, out_2
+):
+    nc = tc.nc
+    with ExitStack() as ctx:
+        pool = ctx.enter_context(tc.tile_pool(name="held", bufs=1))
+        psum = ctx.enter_context(tc.psum_pool(name="psum", bufs=1))
+
+        list_a = pool.tile([P, J // 16], U16, name="list_a")
+        list_b = pool.tile([P, J // 16], U16, name="list_b")
+        xa_rows = xa.rearrange("(p t) c -> p t c", t=PACK)
+        xb_rows = xb.rearrange("(p t) c -> p t c", t=PACK)
+        xa_sb = [pool.tile([P, T], F32, name="xa%d" % t) for t in range(PACK)]
+        xb_sb = [pool.tile([P, 2 * S], F32, name="xb%d" % h) for h in range(2)]
+        hb_sb = pool.tile([P, PACK], F32, name="hb_sb")
+        fk_sb = pool.tile([P, PACK], F32, name="fk_sb")
+        w_raw = pool.tile([P, R], U32, name="w_raw")
+        wb_raw = pool.tile([P, N], U16, name="wb_raw")
+        ws_raw = pool.tile([P, R], U8, name="ws_raw")
+        wbs_raw = pool.tile([P, N], U8, name="wbs_raw")
+        rw_sb = pool.tile([P, G], F32, name="rw_sb")
+        qw_sb = pool.tile([P, Q], F32, name="qw_sb")
+
+        def load_xb(h):
+            nc.sync.dma_start(
+                out=xb_sb[h][:], in_=xb_rows[:, 2 * h : 2 * h + 2, :].rearrange("p t c -> p (t c)")
+            )
+
+        def load_xa(t):
+            nc.sync.dma_start(out=xa_sb[t][:], in_=xa_rows[:, t, :])
+
+        nc.gpsimd.memset(ws_raw[:].bitcast(I32), 0)
+        nc.gpsimd.memset(wbs_raw[:].bitcast(I32), 0)
+        nc.gpsimd.dma_start(out=hb_sb[:], in_=hb.rearrange("(p t) o -> p (t o)", t=PACK))
+        nc.gpsimd.dma_start(out=fk_sb[:], in_=fk.rearrange("(p t) o -> p (t o)", t=PACK))
+        nc.gpsimd.dma_start(out=rw_sb[:], in_=rw[0].partition_broadcast(P))
+        nc.gpsimd.dma_start(out=qw_sb[:], in_=qw[0].partition_broadcast(P))
+        load_scale_rows(nc.scalar, ws_raw, w_scales)
+        load_scale_rows(nc.scalar, wbs_raw, wb_scales)
+        nc.sync.dma_start(list_b[:], offs2)
+        load_xb(0)
+        nc.sync.dma_start(list_a[:], offs)
+        load_xb(1)
+        load_xa(0)
+        nc.sync.dma_start(
+            out=w_raw[:].bitcast(I32), in_=w_words[0].rearrange("p c t -> p (c t)").bitcast(I32)
+        )
+        load_xa(1)
+        nc.sync.dma_start(out=wb_raw[:].bitcast(I32), in_=wb_words[0].bitcast(I32))
+        load_xa(2)
+        load_xa(3)
+
+        picked_b = pool.tile([P, PACK, J], F32, name="picked_b")
+        bounded = pool.tile([P, PACK, J], F32, name="bounded")
+        for t in range(PACK):
+            window = xb_sb[t // 2][:, (t % 2) * S : (t % 2 + 1) * S]
+            nc.scalar.activation(picked_b[:, t, :], window.indirect(list_b[:]), COPY)
+            nc.vector.tensor_scalar(bounded[:, t, :], picked_b[:, t, :], hb_sb[:, t : t + 1], None, ALU.min)
+
+        w_codes = pool.tile([P, R], U32, name="w_codes", align_bytes=64)
+        w_plane = pool.tile([P, R], U8, name="w_plane", align_bytes=64)
+        wb_codes = pool.tile([P, N], U16, name="wb_codes", align_bytes=64)
+        wb_plane = pool.tile([P, N], U8, name="wb_plane", align_bytes=64)
+        nc.vector.tensor_copy(
+            w_codes[:].rearrange("p (t c i) -> p c t i", t=PACK, i=4),
+            w_raw[:].rearrange("p (c i t) -> p c t i", t=PACK, i=4),
+        )
+        for dealt, raw in ((w_plane, ws_raw), (wb_codes, wb_raw), (wb_plane, wbs_raw)):
+            nc.vector.tensor_copy(
+                dealt[:].rearrange("p (t m) -> p t m", t=PACK), raw[:].rearrange("p (m t) -> p t m", t=PACK)
+            )
+        weight = pool.tile([P, 2, Q], F32, name="weight")
+        nc.gpsimd.tensor_tensor(
+            weight[:],
+            rw_sb[:].rearrange("p (q e) -> p e q", e=2),
+            qw_sb[:].unsqueeze(1).to_broadcast([P, 2, Q]),
+            ALU.mult,
+        )
+
+        gap = pool.tile([P, PACK, J], F32, name="gap")
+        u = pool.tile([P, J * PACK], BF16, name="u", align_bytes=64)
+        u_by_t = u[:].rearrange("p (j t) -> p t j", t=PACK)
+        halves = [slice(h * HALF, (h + 1) * HALF) for h in range(2)]
+        for t in range(PACK - 1):
+            nc.vector.tensor_tensor(gap[:, t, :], xa_sb[t][:].indirect(list_a[:]), bounded[:, t, :], ALU.subtract)
+            if t < 2:
+                nc.scalar.activation(u_by_t[:, t, :], gap[:, t, :], COPY, scale=fk_sb[:, t : t + 1])
+            else:
+                nc.vector.tensor_scalar(u_by_t[:, t, :], gap[:, t, :], fk_sb[:, t : t + 1], None, ALU.mult)
+        last = PACK - 1
+        for h in range(2):
+            nc.vector.tensor_tensor(
+                gap[:, last, halves[h]],
+                xa_sb[last][:].indirect(list_a[:, 8 * h : 8 * h + 8]),
+                bounded[:, last, halves[h]],
+                ALU.subtract,
+            )
+        for h in range(2):
+            nc.vector.tensor_scalar(
+                u_by_t[:, last, halves[h]], gap[:, last, halves[h]], fk_sb[:, last : last + 1], None, ALU.mult
+            )
+        u_codes = [pool.tile([P, HALF], U32, name="u_codes%d" % h, align_bytes=64) for h in range(2)]
+        u_plane = [pool.tile([P, HALF], U8, name="u_plane%d" % h, align_bytes=64) for h in range(2)]
+        for h in range(2):
+            nc.vector.quantize_mx(
+                out=u_codes[h][:].bitcast(E5M2),
+                scales=u_plane[h][:],
+                in_=u[:, h * HALF * PACK : (h + 1) * HALF * PACK],
+            )
+
+        hid = pool.tile([P, G * PACK], BF16, name="hid", align_bytes=64)
+        hid_by_t = hid[:].rearrange("p (g t) -> p g t", t=PACK)
+        for h in range(2):
+            for pair in range(2):
+                acc = psum.tile([P, 2, HALF], F32, name="acc%d%d" % (h, pair))
+                for i in range(2):
+                    cols = slice((2 * pair + i) * P, (2 * pair + i + 1) * P)
+                    nc.tensor.matmul_mx(
+                        out=acc[:, i, :],
+                        lhsT=w_codes[:, cols].bitcast(E5M2),
+                        lhsT_scale=w_plane[:, cols],
+                        rhs=u_codes[h][:].bitcast(E5M2),
+                        rhs_scale=u_plane[h][:],
+                        start=True,
+                        stop=True,
+                    )
+                nc.vector.tensor_reduce(
+                    hid_by_t[:, h * G // 2 : (h + 1) * G // 2, 2 * pair : 2 * pair + 2],
+                    acc[:].rearrange("p i (g e) -> p g i e", e=2),
+                    AXIS_X,
+                    ALU.max,
+                )
+        hid_codes = pool.tile([P, G], U32, name="hid_codes", align_bytes=64)
+        hid_plane = pool.tile([P, G], U8, name="hid_plane", align_bytes=64)
+        nc.vector.quantize_mx(out=hid_codes[:].bitcast(E5M2), scales=hid_plane[:], in_=hid[:])
+
+        terms = pool.tile([P, 2, 2, Q, 2], F32, name="terms")
+        for pair in range(2):
+            prod = psum.tile([P, 2, G], F32, name="prod%d" % pair)
+            for i in range(2):
+                cols = slice((2 * pair + i) * P, (2 * pair + i + 1) * P)
+                nc.tensor.matmul_mx(
+                    out=prod[:, i, :],
+                    lhsT=wb_codes[:, cols].bitcast(E2M1),
+                    lhsT_scale=wb_plane[:, cols],
+                    rhs=hid_codes[:].bitcast(E5M2),
+                    rhs_scale=hid_plane[:],
+                    start=True,
+                    stop=True,
+                )
+            nc.vector.tensor_tensor(
+                terms[:, pair],
+                prod[:].rearrange("p i (q e) -> p e q i", e=2),
+                weight[:].unsqueeze(3).to_broadcast([P, 2, Q, 2]),
+                ALU.mult,
+            )
+
+        y = pool.tile([P, PACK, Q], F32, name="y")
+        y_bf = pool.tile([P, Q * PACK], BF16, name="y_bf", align_bytes=64)
+        y_codes = pool.tile([P, Q], U32, name="y_codes", align_bytes=64)
+        y_plane = pool.tile([P, Q], U8, name="y_plane", align_bytes=64)
+        out_rows = out_0.rearrange("(p t) q -> p t q", t=PACK)
+
+        def sum_and_store(pair):
+            rows = slice(2 * pair, 2 * pair + 2)
+            nc.vector.tensor_tensor(
+                y[:, rows, :],
+                terms[:, pair, 0].rearrange("p q i -> p i q"),
+                terms[:, pair, 1].rearrange("p q i -> p i q"),
+                ALU.add,
+            )
+            nc.scalar.dma_start(out=out_rows[:, rows, :], in_=y[:, rows, :])
+
+        sum_and_store(0)
+        nc.vector.tensor_tensor(
+            y_bf[:].rearrange("p (q a i) -> p q a i", a=2, i=2),
+            terms[:, :, 0].rearrange("p a q i -> p q a i"),
+            terms[:, :, 1].rearrange("p a q i -> p q a i"),
+            ALU.add,
+        )
+        sum_and_store(1)
+        nc.vector.quantize_mx(out=y_codes[:].bitcast(E4M3), scales=y_plane[:], in_=y_bf[:])
+        nc.sync.dma_start(
+            out=out_1[0].rearrange("p c t -> p (c t)").bitcast(I32), in_=y_codes[:].bitcast(I32)
+        )
+        for quad in range(4):
+            queue = nc.sync if quad % 2 else nc.scalar
+            queue.dma_start(
+                out=out_2[0, 4 * quad : 4 * quad + 4, :].bitcast(I32),
+                in_=y_plane[32 * quad : 32 * quad + 4, :].bitcast(I32),
+            )

@@ -1,6 +1,7 @@
 from contextlib import ExitStack
 
 import concourse.mybir as mybir
+from concourse.masks import make_identity
 
 K, T, J, S, R, G, N, Q = 512, 1024, 256, 512, 512, 128, 512, 64
 FLOPS = 2 * K * R * J + 2 * R * N * G
@@ -23,12 +24,11 @@ PACK = 4
 HALF = J // 2
 
 
-def load_scale_rows(queue, tile, scales):
-    for quad in range(4):
-        queue.dma_start(
-            out=tile[32 * quad : 32 * quad + 4, :].bitcast(I32),
-            in_=scales[0, 4 * quad : 4 * quad + 4, :].bitcast(I32),
-        )
+def load_scale_rows(queue, tile, scales, quad):
+    queue.dma_start(
+        out=tile[32 * quad : 32 * quad + 4, :].bitcast(I32),
+        in_=scales[0, 4 * quad : 4 * quad + 4, :].bitcast(I32),
+    )
 
 
 def tile_list_boundedgaps_pooled_groupsums_pl_kernel(
@@ -51,8 +51,10 @@ def tile_list_boundedgaps_pooled_groupsums_pl_kernel(
         wb_raw = pool.tile([P, N], U16, name="wb_raw")
         ws_raw = pool.tile([P, R], U8, name="ws_raw")
         wbs_raw = pool.tile([P, N], U8, name="wbs_raw")
-        rw_sb = pool.tile([P, G], F32, name="rw_sb")
-        qw_sb = pool.tile([P, Q], F32, name="qw_sb")
+        rw_sb = pool.tile([Q, 2], F32, name="rw_sb")
+        qw_sb = pool.tile([Q, 1], F32, name="qw_sb")
+        weight_col = pool.tile([P, 2], F32, name="weight_col")
+        ident = pool.tile([P, P], F32, name="ident")
 
         def load_xb(h):
             nc.sync.dma_start(
@@ -62,38 +64,53 @@ def tile_list_boundedgaps_pooled_groupsums_pl_kernel(
         def load_xa(t):
             nc.sync.dma_start(out=xa_sb[t][:], in_=xa_rows[:, t, :])
 
-        nc.gpsimd.memset(ws_raw[:].bitcast(I32), 0)
         nc.gpsimd.memset(wbs_raw[:].bitcast(I32), 0)
-        nc.gpsimd.dma_start(out=hb_sb[:], in_=hb.rearrange("(p t) o -> p (t o)", t=PACK))
-        nc.gpsimd.dma_start(out=fk_sb[:], in_=fk.rearrange("(p t) o -> p (t o)", t=PACK))
-        nc.gpsimd.dma_start(out=rw_sb[:], in_=rw[0].partition_broadcast(P))
-        nc.gpsimd.dma_start(out=qw_sb[:], in_=qw[0].partition_broadcast(P))
-        load_scale_rows(nc.scalar, ws_raw, w_scales)
-        load_scale_rows(nc.scalar, wbs_raw, wb_scales)
-        nc.sync.dma_start(list_b[:], offs2)
-        load_xb(0)
-        nc.sync.dma_start(list_a[:], offs)
-        load_xb(1)
-        load_xa(0)
+        nc.gpsimd.memset(ws_raw[:].bitcast(I32), 0)
+        nc.gpsimd.memset(weight_col[:], 0.0)
+        make_identity(nc, ident[:])
+        for quad in range(4):
+            load_scale_rows(nc.gpsimd, wbs_raw, wb_scales, quad)
+        nc.scalar.dma_start(out=rw_sb[:], in_=rw.rearrange("o (q e) -> q (o e)", e=2))
+        nc.scalar.dma_start(out=qw_sb[:], in_=qw.rearrange("o q -> q o"))
+        nc.scalar.dma_start(out=hb_sb[:], in_=hb.rearrange("(p t) o -> p (t o)", t=PACK))
+        nc.scalar.dma_start(out=fk_sb[:], in_=fk.rearrange("(p t) o -> p (t o)", t=PACK))
         nc.sync.dma_start(
             out=w_raw[:].bitcast(I32), in_=w_words[0].rearrange("p c t -> p (c t)").bitcast(I32)
         )
-        load_xa(1)
+        load_xb(0)
         nc.sync.dma_start(out=wb_raw[:].bitcast(I32), in_=wb_words[0].bitcast(I32))
+        nc.sync.dma_start(list_b[:], offs2)
+        load_xb(1)
+        load_xa(0)
+        nc.sync.dma_start(list_a[:], offs)
+        load_scale_rows(nc.sync, ws_raw, w_scales, 0)
+        load_xa(1)
+        for quad in range(1, 4):
+            load_scale_rows(nc.sync, ws_raw, w_scales, quad)
         load_xa(2)
         load_xa(3)
 
-        picked_b = pool.tile([P, PACK, J], F32, name="picked_b")
+        nc.scalar.activation(weight_col[0:Q, :], rw_sb[:], COPY, scale=qw_sb[:])
+        spread = psum.tile([P, 2, P], F32, name="spread")
+        for e in range(2):
+            nc.tensor.transpose(spread[:, e, :], weight_col[:, e : e + 1].to_broadcast([P, P]), ident[:])
+        weight = pool.tile([P, 2, Q], F32, name="weight")
+        nc.scalar.activation(weight[:], spread[:, :, 0:Q], COPY)
+
+        picked_b = [pool.tile([P, J], F32, name="picked_b%d" % t, align_bytes=64) for t in range(PACK)]
         bounded = pool.tile([P, PACK, J], F32, name="bounded")
         for t in range(PACK):
             window = xb_sb[t // 2][:, (t % 2) * S : (t % 2 + 1) * S]
-            nc.scalar.activation(picked_b[:, t, :], window.indirect(list_b[:]), COPY)
-            nc.vector.tensor_scalar(bounded[:, t, :], picked_b[:, t, :], hb_sb[:, t : t + 1], None, ALU.min)
+            if t == 0:
+                nc.vector.tensor_copy(picked_b[t][:], window.indirect(list_b[:]))
+            else:
+                nc.scalar.activation(picked_b[t][:], window.indirect(list_b[:]), COPY)
+            nc.vector.tensor_scalar(bounded[:, t, :], picked_b[t][:], hb_sb[:, t : t + 1], None, ALU.min)
 
         w_codes = pool.tile([P, R], U32, name="w_codes", align_bytes=64)
         w_plane = pool.tile([P, R], U8, name="w_plane", align_bytes=64)
         wb_codes = pool.tile([P, N], U16, name="wb_codes", align_bytes=64)
-        wb_plane = pool.tile([P, N], U8, name="wb_plane", align_bytes=64)
+        wb_plane = pool.tile([P, N], U8, name="wb_plane", tag="picked_b3", align_bytes=64)
         nc.vector.tensor_copy(
             w_codes[:].rearrange("p (t c i) -> p c t i", t=PACK, i=4),
             w_raw[:].rearrange("p (c i t) -> p c t i", t=PACK, i=4),
@@ -102,36 +119,21 @@ def tile_list_boundedgaps_pooled_groupsums_pl_kernel(
             nc.vector.tensor_copy(
                 dealt[:].rearrange("p (t m) -> p t m", t=PACK), raw[:].rearrange("p (m t) -> p t m", t=PACK)
             )
-        weight = pool.tile([P, 2, Q], F32, name="weight")
-        nc.gpsimd.tensor_tensor(
-            weight[:],
-            rw_sb[:].rearrange("p (q e) -> p e q", e=2),
-            qw_sb[:].unsqueeze(1).to_broadcast([P, 2, Q]),
-            ALU.mult,
-        )
 
         gap = pool.tile([P, PACK, J], F32, name="gap")
         u = pool.tile([P, J * PACK], BF16, name="u", align_bytes=64)
         u_by_t = u[:].rearrange("p (j t) -> p t j", t=PACK)
         halves = [slice(h * HALF, (h + 1) * HALF) for h in range(2)]
-        for t in range(PACK - 1):
-            nc.vector.tensor_tensor(gap[:, t, :], xa_sb[t][:].indirect(list_a[:]), bounded[:, t, :], ALU.subtract)
-            if t < 2:
-                nc.scalar.activation(u_by_t[:, t, :], gap[:, t, :], COPY, scale=fk_sb[:, t : t + 1])
-            else:
-                nc.vector.tensor_scalar(u_by_t[:, t, :], gap[:, t, :], fk_sb[:, t : t + 1], None, ALU.mult)
-        last = PACK - 1
-        for h in range(2):
-            nc.vector.tensor_tensor(
-                gap[:, last, halves[h]],
-                xa_sb[last][:].indirect(list_a[:, 8 * h : 8 * h + 8]),
-                bounded[:, last, halves[h]],
-                ALU.subtract,
-            )
-        for h in range(2):
-            nc.vector.tensor_scalar(
-                u_by_t[:, last, halves[h]], gap[:, last, halves[h]], fk_sb[:, last : last + 1], None, ALU.mult
-            )
+        for t in range(PACK):
+            pieces = [slice(0, J)] if t < 2 else halves
+            for cols in pieces:
+                nc.vector.tensor_tensor(
+                    gap[:, t, cols],
+                    xa_sb[t][:].indirect(list_a[:, cols.start // 16 : cols.stop // 16]),
+                    bounded[:, t, cols],
+                    ALU.subtract,
+                )
+                nc.scalar.activation(u_by_t[:, t, cols], gap[:, t, cols], COPY, scale=fk_sb[:, t : t + 1])
         u_codes = [pool.tile([P, HALF], U32, name="u_codes%d" % h, align_bytes=64) for h in range(2)]
         u_plane = [pool.tile([P, HALF], U8, name="u_plane%d" % h, align_bytes=64) for h in range(2)]
         for h in range(2):

@@ -43,11 +43,11 @@ def tile_list_boundedgaps_pooled_groupsums_pl_kernel(
         list_b = pool.tile([P, J // 16], U16, name="list_b")
         xa_rows = xa.rearrange("(p t) c -> p t c", t=PACK)
         xb_rows = xb.rearrange("(p t) c -> p t c", t=PACK)
-        xa_sb = [pool.tile([P, T], F32, name="xa%d" % t) for t in range(PACK)]
+        xa_sb = [pool.tile([P, T], F32, name="xa%d" % t, align_bytes=64) for t in range(PACK)]
         xb_sb = [pool.tile([P, 2 * S], F32, name="xb%d" % h) for h in range(2)]
         hb_sb = pool.tile([P, PACK], F32, name="hb_sb")
         fk_sb = pool.tile([P, PACK], F32, name="fk_sb")
-        w_raw = pool.tile([P, R], U32, name="w_raw")
+        w_raw = pool.tile([P, R], U32, name="w_raw", align_bytes=64)
         wb_raw = pool.tile([P, N], U16, name="wb_raw")
         ws_raw = pool.tile([P, R], U8, name="ws_raw")
         wbs_raw = pool.tile([P, N], U8, name="wbs_raw")
@@ -65,30 +65,32 @@ def tile_list_boundedgaps_pooled_groupsums_pl_kernel(
             nc.sync.dma_start(out=xa_sb[t][:], in_=xa_rows[:, t, :])
 
         nc.gpsimd.memset(wbs_raw[:].bitcast(I32), 0)
-        nc.gpsimd.memset(ws_raw[:].bitcast(I32), 0)
-        nc.gpsimd.memset(weight_col[:], 0.0)
-        make_identity(nc, ident[:])
+        nc.vector.memset(ident[:], 0.0)
+        nc.vector.memset(ws_raw[:].bitcast(I32), 0)
+        nc.vector.memset(weight_col[:], 0.0)
+        make_identity(nc, ident[:], nomemset=True)
         for quad in range(4):
             load_scale_rows(nc.gpsimd, wbs_raw, wb_scales, quad)
         nc.scalar.dma_start(out=rw_sb[:], in_=rw.rearrange("o (q e) -> q (o e)", e=2))
         nc.scalar.dma_start(out=qw_sb[:], in_=qw.rearrange("o q -> q o"))
         nc.scalar.dma_start(out=hb_sb[:], in_=hb.rearrange("(p t) o -> p (t o)", t=PACK))
         nc.scalar.dma_start(out=fk_sb[:], in_=fk.rearrange("(p t) o -> p (t o)", t=PACK))
+        nc.sync.dma_start(out=wb_raw[:].bitcast(I32), in_=wb_words[0].bitcast(I32))
+        load_xb(0)
+        nc.sync.dma_start(list_b[:], offs2)
+        load_xa(0)
+        nc.sync.dma_start(list_a[:], offs)
+        load_xa(1)
+        load_scale_rows(nc.sync, ws_raw, w_scales, 0)
+        load_scale_rows(nc.sync, ws_raw, w_scales, 1)
+        load_xb(1)
+        load_scale_rows(nc.sync, ws_raw, w_scales, 2)
+        load_scale_rows(nc.sync, ws_raw, w_scales, 3)
+        load_xa(2)
+        load_xa(3)
         nc.sync.dma_start(
             out=w_raw[:].bitcast(I32), in_=w_words[0].rearrange("p c t -> p (c t)").bitcast(I32)
         )
-        load_xb(0)
-        nc.sync.dma_start(out=wb_raw[:].bitcast(I32), in_=wb_words[0].bitcast(I32))
-        nc.sync.dma_start(list_b[:], offs2)
-        load_xb(1)
-        load_xa(0)
-        nc.sync.dma_start(list_a[:], offs)
-        load_scale_rows(nc.sync, ws_raw, w_scales, 0)
-        load_xa(1)
-        for quad in range(1, 4):
-            load_scale_rows(nc.sync, ws_raw, w_scales, quad)
-        load_xa(2)
-        load_xa(3)
 
         nc.scalar.activation(weight_col[0:Q, :], rw_sb[:], COPY, scale=qw_sb[:])
         spread = psum.tile([P, 2, P], F32, name="spread")
@@ -97,34 +99,27 @@ def tile_list_boundedgaps_pooled_groupsums_pl_kernel(
         weight = pool.tile([P, 2, Q], F32, name="weight")
         nc.scalar.activation(weight[:], spread[:, :, 0:Q], COPY)
 
-        picked_b = [pool.tile([P, J], F32, name="picked_b%d" % t, align_bytes=64) for t in range(PACK)]
-        bounded = pool.tile([P, PACK, J], F32, name="bounded")
-        for t in range(PACK):
+        def deal(dealt, raw):
+            nc.vector.tensor_copy(
+                dealt[:].rearrange("p (t m) -> p t m", t=PACK), raw[:].rearrange("p (m t) -> p t m", t=PACK)
+            )
+
+        picked_b = [pool.tile([P, J], F32, name="picked_b%d" % t) for t in range(PACK)]
+        bounded = pool.tile([P, PACK, J], F32, name="bounded", align_bytes=64)
+        gap = pool.tile([P, PACK, J], F32, name="gap")
+        u = pool.tile([P, J * PACK], BF16, name="u", align_bytes=64)
+        u_by_t = u[:].rearrange("p (j t) -> p t j", t=PACK)
+        halves = [slice(h * HALF, (h + 1) * HALF) for h in range(2)]
+
+        def bound(t):
             window = xb_sb[t // 2][:, (t % 2) * S : (t % 2 + 1) * S]
-            if t == 0:
+            if t % 2 == 0:
                 nc.vector.tensor_copy(picked_b[t][:], window.indirect(list_b[:]))
             else:
                 nc.scalar.activation(picked_b[t][:], window.indirect(list_b[:]), COPY)
             nc.vector.tensor_scalar(bounded[:, t, :], picked_b[t][:], hb_sb[:, t : t + 1], None, ALU.min)
 
-        w_codes = pool.tile([P, R], U32, name="w_codes", align_bytes=64)
-        w_plane = pool.tile([P, R], U8, name="w_plane", align_bytes=64)
-        wb_codes = pool.tile([P, N], U16, name="wb_codes", align_bytes=64)
-        wb_plane = pool.tile([P, N], U8, name="wb_plane", tag="picked_b3", align_bytes=64)
-        nc.vector.tensor_copy(
-            w_codes[:].rearrange("p (t c i) -> p c t i", t=PACK, i=4),
-            w_raw[:].rearrange("p (c i t) -> p c t i", t=PACK, i=4),
-        )
-        for dealt, raw in ((w_plane, ws_raw), (wb_codes, wb_raw), (wb_plane, wbs_raw)):
-            nc.vector.tensor_copy(
-                dealt[:].rearrange("p (t m) -> p t m", t=PACK), raw[:].rearrange("p (m t) -> p t m", t=PACK)
-            )
-
-        gap = pool.tile([P, PACK, J], F32, name="gap")
-        u = pool.tile([P, J * PACK], BF16, name="u", align_bytes=64)
-        u_by_t = u[:].rearrange("p (j t) -> p t j", t=PACK)
-        halves = [slice(h * HALF, (h + 1) * HALF) for h in range(2)]
-        for t in range(PACK):
+        def difference(t):
             pieces = [slice(0, J)] if t < 2 else halves
             for cols in pieces:
                 nc.vector.tensor_tensor(
@@ -134,7 +129,30 @@ def tile_list_boundedgaps_pooled_groupsums_pl_kernel(
                     ALU.subtract,
                 )
                 nc.scalar.activation(u_by_t[:, t, cols], gap[:, t, cols], COPY, scale=fk_sb[:, t : t + 1])
-        u_codes = [pool.tile([P, HALF], U32, name="u_codes%d" % h, align_bytes=64) for h in range(2)]
+
+        wb_codes = pool.tile([P, N], U16, name="wb_codes", align_bytes=64)
+        deal(wb_codes, wb_raw)
+        bound(0)
+        bound(1)
+        difference(0)
+        difference(1)
+        w_plane = pool.tile([P, R], U8, name="w_plane", align_bytes=64)
+        deal(w_plane, ws_raw)
+        wb_plane = pool.tile([P, N], U8, name="wb_plane", tag="xa1", align_bytes=64)
+        deal(wb_plane, wbs_raw)
+        bound(2)
+        bound(3)
+        difference(2)
+        difference(3)
+        w_codes = pool.tile([P, R], U32, name="w_codes", tag="bounded", align_bytes=64)
+        nc.vector.tensor_copy(
+            w_codes[:].rearrange("p (t c i) -> p c t i", t=PACK, i=4),
+            w_raw[:].rearrange("p (c i t) -> p c t i", t=PACK, i=4),
+        )
+        u_codes = [
+            pool.tile([P, HALF], U32, name="u_codes0", tag="w_raw", align_bytes=64),
+            pool.tile([P, HALF], U32, name="u_codes1", align_bytes=64),
+        ]
         u_plane = [pool.tile([P, HALF], U8, name="u_plane%d" % h, align_bytes=64) for h in range(2)]
         for h in range(2):
             nc.vector.quantize_mx(

@@ -47,7 +47,7 @@ def tile_list_boundedgaps_pooled_groupsums_pl_kernel(
         xb_sb = [pool.tile([P, 2 * S], F32, name="xb%d" % h) for h in range(2)]
         hb_sb = pool.tile([P, PACK], F32, name="hb_sb")
         fk_sb = pool.tile([P, PACK], F32, name="fk_sb")
-        w_raw = pool.tile([P, R], U32, name="w_raw", align_bytes=64)
+        w_raw = pool.tile([P, R], U32, name="w_raw")
         wb_raw = pool.tile([P, N], U16, name="wb_raw")
         ws_raw = pool.tile([P, R], U8, name="ws_raw")
         wbs_raw = pool.tile([P, N], U8, name="wbs_raw")
@@ -64,28 +64,27 @@ def tile_list_boundedgaps_pooled_groupsums_pl_kernel(
         def load_xa(t):
             nc.sync.dma_start(out=xa_sb[t][:], in_=xa_rows[:, t, :])
 
+        nc.gpsimd.memset(ws_raw[:].bitcast(I32), 0)
         nc.gpsimd.memset(wbs_raw[:].bitcast(I32), 0)
         nc.vector.memset(ident[:], 0.0)
-        nc.vector.memset(ws_raw[:].bitcast(I32), 0)
         nc.vector.memset(weight_col[:], 0.0)
         make_identity(nc, ident[:], nomemset=True)
         for quad in range(4):
             load_scale_rows(nc.gpsimd, wbs_raw, wb_scales, quad)
         nc.scalar.dma_start(out=rw_sb[:], in_=rw.rearrange("o (q e) -> q (o e)", e=2))
         nc.scalar.dma_start(out=qw_sb[:], in_=qw.rearrange("o q -> q o"))
-        nc.scalar.dma_start(out=hb_sb[:], in_=hb.rearrange("(p t) o -> p (t o)", t=PACK))
-        nc.scalar.dma_start(out=fk_sb[:], in_=fk.rearrange("(p t) o -> p (t o)", t=PACK))
         nc.sync.dma_start(out=wb_raw[:].bitcast(I32), in_=wb_words[0].bitcast(I32))
+        nc.sync.dma_start(out=hb_sb[:], in_=hb.rearrange("(p t) o -> p (t o)", t=PACK))
         load_xb(0)
         nc.sync.dma_start(list_b[:], offs2)
+        load_xb(1)
+        nc.sync.dma_start(out=fk_sb[:], in_=fk.rearrange("(p t) o -> p (t o)", t=PACK))
         load_xa(0)
         nc.sync.dma_start(list_a[:], offs)
-        load_xa(1)
         load_scale_rows(nc.sync, ws_raw, w_scales, 0)
-        load_scale_rows(nc.sync, ws_raw, w_scales, 1)
-        load_xb(1)
-        load_scale_rows(nc.sync, ws_raw, w_scales, 2)
-        load_scale_rows(nc.sync, ws_raw, w_scales, 3)
+        load_xa(1)
+        for quad in range(1, 4):
+            load_scale_rows(nc.sync, ws_raw, w_scales, quad)
         load_xa(2)
         load_xa(3)
         nc.sync.dma_start(
@@ -104,55 +103,48 @@ def tile_list_boundedgaps_pooled_groupsums_pl_kernel(
                 dealt[:].rearrange("p (t m) -> p t m", t=PACK), raw[:].rearrange("p (m t) -> p t m", t=PACK)
             )
 
-        picked_b = [pool.tile([P, J], F32, name="picked_b%d" % t) for t in range(PACK)]
-        bounded = pool.tile([P, PACK, J], F32, name="bounded", align_bytes=64)
-        gap = pool.tile([P, PACK, J], F32, name="gap")
         u = pool.tile([P, J * PACK], BF16, name="u", align_bytes=64)
         u_by_t = u[:].rearrange("p (j t) -> p t j", t=PACK)
         halves = [slice(h * HALF, (h + 1) * HALF) for h in range(2)]
 
         def bound(t):
+            picked = pool.tile([P, J], F32, name="picked%d" % t)
             window = xb_sb[t // 2][:, (t % 2) * S : (t % 2 + 1) * S]
             if t % 2 == 0:
-                nc.vector.tensor_copy(picked_b[t][:], window.indirect(list_b[:]))
+                nc.vector.tensor_copy(picked[:], window.indirect(list_b[:]))
             else:
-                nc.scalar.activation(picked_b[t][:], window.indirect(list_b[:]), COPY)
-            nc.vector.tensor_scalar(bounded[:, t, :], picked_b[t][:], hb_sb[:, t : t + 1], None, ALU.min)
+                nc.scalar.activation(picked[:], window.indirect(list_b[:]), COPY)
+            bounded = pool.tile([P, J], F32, name="bounded%d" % t, align_bytes=64)
+            nc.vector.tensor_scalar(bounded[:], picked[:], hb_sb[:, t : t + 1], None, ALU.min)
+            return bounded
 
-        def difference(t):
+        def difference(t, bounded, tag):
+            gap = pool.tile([P, J], F32, name="gap%d" % t, tag=tag, align_bytes=64)
             pieces = [slice(0, J)] if t < 2 else halves
             for cols in pieces:
                 nc.vector.tensor_tensor(
-                    gap[:, t, cols],
+                    gap[:, cols],
                     xa_sb[t][:].indirect(list_a[:, cols.start // 16 : cols.stop // 16]),
-                    bounded[:, t, cols],
+                    bounded[:, cols],
                     ALU.subtract,
                 )
-                nc.scalar.activation(u_by_t[:, t, cols], gap[:, t, cols], COPY, scale=fk_sb[:, t : t + 1])
+                nc.scalar.activation(u_by_t[:, t, cols], gap[:, cols], COPY, scale=fk_sb[:, t : t + 1])
 
         wb_codes = pool.tile([P, N], U16, name="wb_codes", align_bytes=64)
         deal(wb_codes, wb_raw)
-        bound(0)
-        bound(1)
-        difference(0)
-        difference(1)
-        w_plane = pool.tile([P, R], U8, name="w_plane", align_bytes=64)
+        bounded = [bound(t) for t in range(PACK)]
+        difference(0, bounded[0], "gap0")
+        difference(1, bounded[1], "bounded0")
+        w_plane = pool.tile([P, R], U8, name="w_plane", tag="xa1", align_bytes=64)
         deal(w_plane, ws_raw)
-        wb_plane = pool.tile([P, N], U8, name="wb_plane", tag="xa1", align_bytes=64)
-        deal(wb_plane, wbs_raw)
-        bound(2)
-        bound(3)
-        difference(2)
-        difference(3)
-        w_codes = pool.tile([P, R], U32, name="w_codes", tag="bounded", align_bytes=64)
+        difference(2, bounded[2], "bounded1")
+        difference(3, bounded[3], "bounded2")
+        w_codes = pool.tile([P, R], U32, name="w_codes", tag="bounded3", align_bytes=64)
         nc.vector.tensor_copy(
             w_codes[:].rearrange("p (t c i) -> p c t i", t=PACK, i=4),
             w_raw[:].rearrange("p (c i t) -> p c t i", t=PACK, i=4),
         )
-        u_codes = [
-            pool.tile([P, HALF], U32, name="u_codes0", tag="w_raw", align_bytes=64),
-            pool.tile([P, HALF], U32, name="u_codes1", align_bytes=64),
-        ]
+        u_codes = [pool.tile([P, HALF], U32, name="u_codes%d" % h, align_bytes=64) for h in range(2)]
         u_plane = [pool.tile([P, HALF], U8, name="u_plane%d" % h, align_bytes=64) for h in range(2)]
         for h in range(2):
             nc.vector.quantize_mx(
@@ -183,6 +175,8 @@ def tile_list_boundedgaps_pooled_groupsums_pl_kernel(
                     AXIS_X,
                     ALU.max,
                 )
+        wb_plane = pool.tile([P, N], U8, name="wb_plane", tag="u_codes1", align_bytes=64)
+        deal(wb_plane, wbs_raw)
         hid_codes = pool.tile([P, G], U32, name="hid_codes", align_bytes=64)
         hid_plane = pool.tile([P, G], U8, name="hid_plane", align_bytes=64)
         nc.vector.quantize_mx(out=hid_codes[:].bitcast(E5M2), scales=hid_plane[:], in_=hid[:])

from contextlib import ExitStack

import concourse.mybir as mybir
from concourse.masks import make_identity

K, T, J, S, R, G, N, Q = 512, 1024, 256, 512, 512, 128, 512, 64
FLOPS = 2 * K * R * J + 2 * R * N * G

F32 = mybir.dt.float32
BF16 = mybir.dt.bfloat16
I32 = mybir.dt.int32
U32 = mybir.dt.uint32
U16 = mybir.dt.uint16
U8 = mybir.dt.uint8
E5M2 = mybir.dt.float8_e5m2_x4
E4M3 = mybir.dt.float8_e4m3fn_x4
E2M1 = mybir.dt.float4_e2m1fn_x4
ALU = mybir.AluOpType
COPY = mybir.ActivationFunctionType.Copy
AXIS_X = mybir.AxisListType.X

P = 128
PACK = 4
HALF = J // 2


def load_scale_rows(queue, tile, scales, quad):
    queue.dma_start(
        out=tile[32 * quad : 32 * quad + 4, :].bitcast(I32),
        in_=scales[0, 4 * quad : 4 * quad + 4, :].bitcast(I32),
    )


def tile_list_boundedgaps_pooled_groupsums_pl_kernel(
    tc, xa, xb, hb, fk, w_words, w_scales, wb_words, wb_scales, rw, qw, offs, offs2, out_0, out_1, out_2
):
    nc = tc.nc
    with ExitStack() as ctx:
        pool = ctx.enter_context(tc.tile_pool(name="held", bufs=1))
        psum = ctx.enter_context(tc.psum_pool(name="psum", bufs=1))

        list_a = pool.tile([P, J // 16], U16, name="list_a")
        list_b = pool.tile([P, J // 16], U16, name="list_b")
        xa_rows = xa.rearrange("(p t) c -> p t c", t=PACK)
        xb_rows = xb.rearrange("(p t) c -> p t c", t=PACK)
        xa_sb = [pool.tile([P, T], F32, name="xa%d" % t, align_bytes=64) for t in range(PACK)]
        xb_sb = [pool.tile([P, 2 * S], F32, name="xb%d" % h) for h in range(2)]
        hb_sb = pool.tile([P, PACK], F32, name="hb_sb")
        fk_sb = pool.tile([P, PACK], F32, name="fk_sb")
        w_raw = pool.tile([P, R], U32, name="w_raw")
        wb_raw = pool.tile([P, N], U16, name="wb_raw")
        ws_raw = pool.tile([P, R], U8, name="ws_raw")
        wbs_raw = pool.tile([P, N], U8, name="wbs_raw")
        rw_sb = pool.tile([Q, 2], F32, name="rw_sb")
        qw_sb = pool.tile([Q, 1], F32, name="qw_sb")
        weight_col = pool.tile([P, 2], F32, name="weight_col")
        ident = pool.tile([P, P], F32, name="ident")

        def load_xb(h):
            nc.sync.dma_start(
                out=xb_sb[h][:], in_=xb_rows[:, 2 * h : 2 * h + 2, :].rearrange("p t c -> p (t c)")
            )

        def load_xa(t):
            nc.sync.dma_start(out=xa_sb[t][:], in_=xa_rows[:, t, :])

        nc.gpsimd.memset(ws_raw[:].bitcast(I32), 0)
        nc.gpsimd.memset(wbs_raw[:].bitcast(I32), 0)
        nc.vector.memset(ident[:], 0.0)
        nc.vector.memset(weight_col[:], 0.0)
        make_identity(nc, ident[:], nomemset=True)
        for quad in range(4):
            load_scale_rows(nc.gpsimd, wbs_raw, wb_scales, quad)
        nc.scalar.dma_start(out=rw_sb[:], in_=rw.rearrange("o (q e) -> q (o e)", e=2))
        nc.scalar.dma_start(out=qw_sb[:], in_=qw.rearrange("o q -> q o"))
        nc.sync.dma_start(out=wb_raw[:].bitcast(I32), in_=wb_words[0].bitcast(I32))
        nc.sync.dma_start(out=hb_sb[:], in_=hb.rearrange("(p t) o -> p (t o)", t=PACK))
        load_xb(0)
        nc.sync.dma_start(list_b[:], offs2)
        load_xb(1)
        nc.sync.dma_start(out=fk_sb[:], in_=fk.rearrange("(p t) o -> p (t o)", t=PACK))
        load_xa(0)
        nc.sync.dma_start(list_a[:], offs)
        load_scale_rows(nc.sync, ws_raw, w_scales, 0)
        load_xa(1)
        for quad in range(1, 4):
            load_scale_rows(nc.sync, ws_raw, w_scales, quad)
        load_xa(2)
        load_xa(3)
        nc.sync.dma_start(
            out=w_raw[:].bitcast(I32), in_=w_words[0].rearrange("p c t -> p (c t)").bitcast(I32)
        )

        nc.scalar.activation(weight_col[0:Q, :], rw_sb[:], COPY, scale=qw_sb[:])
        spread = psum.tile([P, 2, P], F32, name="spread")
        for e in range(2):
            nc.tensor.transpose(spread[:, e, :], weight_col[:, e : e + 1].to_broadcast([P, P]), ident[:])
        weight = pool.tile([P, 2, Q], F32, name="weight")
        nc.scalar.activation(weight[:], spread[:, :, 0:Q], COPY)

        def deal(dealt, raw):
            nc.vector.tensor_copy(
                dealt[:].rearrange("p (t m) -> p t m", t=PACK), raw[:].rearrange("p (m t) -> p t m", t=PACK)
            )

        u = pool.tile([P, J * PACK], BF16, name="u", align_bytes=64)
        u_by_t = u[:].rearrange("p (j t) -> p t j", t=PACK)
        halves = [slice(h * HALF, (h + 1) * HALF) for h in range(2)]

        def bound(t):
            picked = pool.tile([P, J], F32, name="picked%d" % t)
            window = xb_sb[t // 2][:, (t % 2) * S : (t % 2 + 1) * S]
            if t % 2 == 0:
                nc.vector.tensor_copy(picked[:], window.indirect(list_b[:]))
            else:
                nc.scalar.activation(picked[:], window.indirect(list_b[:]), COPY)
            bounded = pool.tile([P, J], F32, name="bounded%d" % t, align_bytes=64)
            nc.vector.tensor_scalar(bounded[:], picked[:], hb_sb[:, t : t + 1], None, ALU.min)
            return bounded

        def difference(t, bounded, tag):
            gap = pool.tile([P, J], F32, name="gap%d" % t, tag=tag, align_bytes=64)
            pieces = [slice(0, J)] if t < 2 else halves
            for cols in pieces:
                nc.vector.tensor_tensor(
                    gap[:, cols],
                    xa_sb[t][:].indirect(list_a[:, cols.start // 16 : cols.stop // 16]),
                    bounded[:, cols],
                    ALU.subtract,
                )
                nc.scalar.activation(u_by_t[:, t, cols], gap[:, cols], COPY, scale=fk_sb[:, t : t + 1])

        wb_codes = pool.tile([P, N], U16, name="wb_codes", align_bytes=64)
        deal(wb_codes, wb_raw)
        bounded = [bound(t) for t in range(PACK)]
        difference(0, bounded[0], "gap0")
        difference(1, bounded[1], "bounded0")
        w_plane = pool.tile([P, R], U8, name="w_plane", tag="xa1", align_bytes=64)
        deal(w_plane, ws_raw)
        difference(2, bounded[2], "bounded1")
        difference(3, bounded[3], "bounded2")
        w_codes = pool.tile([P, R], U32, name="w_codes", tag="bounded3", align_bytes=64)
        nc.vector.tensor_copy(
            w_codes[:].rearrange("p (t c i) -> p c t i", t=PACK, i=4),
            w_raw[:].rearrange("p (c i t) -> p c t i", t=PACK, i=4),
        )
        u_codes = [pool.tile([P, HALF], U32, name="u_codes%d" % h, align_bytes=64) for h in range(2)]
        u_plane = [pool.tile([P, HALF], U8, name="u_plane%d" % h, align_bytes=64) for h in range(2)]
        for h in range(2):
            nc.vector.quantize_mx(
                out=u_codes[h][:].bitcast(E5M2),
                scales=u_plane[h][:],
                in_=u[:, h * HALF * PACK : (h + 1) * HALF * PACK],
            )

        hid = pool.tile([P, G * PACK], BF16, name="hid", align_bytes=64)
        hid_by_t = hid[:].rearrange("p (g t) -> p g t", t=PACK)
        for h in range(2):
            for pair in range(2):
                acc = psum.tile([P, 2, HALF], F32, name="acc%d%d" % (h, pair))
                for i in range(2):
                    cols = slice((2 * pair + i) * P, (2 * pair + i + 1) * P)
                    nc.tensor.matmul_mx(
                        out=acc[:, i, :],
                        lhsT=w_codes[:, cols].bitcast(E5M2),
                        lhsT_scale=w_plane[:, cols],
                        rhs=u_codes[h][:].bitcast(E5M2),
                        rhs_scale=u_plane[h][:],
                        start=True,
                        stop=True,
                    )
                nc.vector.tensor_reduce(
                    hid_by_t[:, h * G // 2 : (h + 1) * G // 2, 2 * pair : 2 * pair + 2],
                    acc[:].rearrange("p i (g e) -> p g i e", e=2),
                    AXIS_X,
                    ALU.max,
                )
        wb_plane = pool.tile([P, N], U8, name="wb_plane", tag="u_codes1", align_bytes=64)
        deal(wb_plane, wbs_raw)
        hid_codes = pool.tile([P, G], U32, name="hid_codes", align_bytes=64)
        hid_plane = pool.tile([P, G], U8, name="hid_plane", align_bytes=64)
        nc.vector.quantize_mx(out=hid_codes[:].bitcast(E5M2), scales=hid_plane[:], in_=hid[:])

        terms = pool.tile([P, 2, 2, Q, 2], F32, name="terms")
        for pair in range(2):
            prod = psum.tile([P, 2, G], F32, name="prod%d" % pair)
            for i in range(2):
                cols = slice((2 * pair + i) * P, (2 * pair + i + 1) * P)
                nc.tensor.matmul_mx(
                    out=prod[:, i, :],
                    lhsT=wb_codes[:, cols].bitcast(E2M1),
                    lhsT_scale=wb_plane[:, cols],
                    rhs=hid_codes[:].bitcast(E5M2),
                    rhs_scale=hid_plane[:],
                    start=True,
                    stop=True,
                )
            nc.vector.tensor_tensor(
                terms[:, pair],
                prod[:].rearrange("p i (q e) -> p e q i", e=2),
                weight[:].unsqueeze(3).to_broadcast([P, 2, Q, 2]),
                ALU.mult,
            )

        y = pool.tile([P, PACK, Q], F32, name="y")
        y_bf = pool.tile([P, Q * PACK], BF16, name="y_bf", align_bytes=64)
        y_codes = pool.tile([P, Q], U32, name="y_codes", align_bytes=64)
        y_plane = pool.tile([P, Q], U8, name="y_plane", align_bytes=64)
        out_rows = out_0.rearrange("(p t) q -> p t q", t=PACK)

        def sum_and_store(pair):
            rows = slice(2 * pair, 2 * pair + 2)
            nc.vector.tensor_tensor(
                y[:, rows, :],
                terms[:, pair, 0].rearrange("p q i -> p i q"),
                terms[:, pair, 1].rearrange("p q i -> p i q"),
                ALU.add,
            )
            nc.scalar.dma_start(out=out_rows[:, rows, :], in_=y[:, rows, :])

        sum_and_store(0)
        nc.vector.tensor_tensor(
            y_bf[:].rearrange("p (q a i) -> p q a i", a=2, i=2),
            terms[:, :, 0].rearrange("p a q i -> p q a i"),
            terms[:, :, 1].rearrange("p a q i -> p q a i"),
            ALU.add,
        )
        sum_and_store(1)
        nc.vector.quantize_mx(out=y_codes[:].bitcast(E4M3), scales=y_plane[:], in_=y_bf[:])
        nc.sync.dma_start(
            out=out_1[0].rearrange("p c t -> p (c t)").bitcast(I32), in_=y_codes[:].bitcast(I32)
        )
        for quad in range(4):
            queue = nc.sync if quad % 2 else nc.scalar
            queue.dma_start(
                out=out_2[0, 4 * quad : 4 * quad + 4, :].bitcast(I32),
                in_=y_plane[32 * quad : 32 * quad + 4, :].bitcast(I32),
            )
